import numpy as np
import ml_dtypes


def mxq(x, axis, fmt="e4m3"):
    dtype, down = {"e4m3": (ml_dtypes.float8_e4m3fn, 7), "e5m2": (ml_dtypes.float8_e5m2, 14)}[fmt]
    v = np.moveaxis(np.asarray(x, np.float32).astype(ml_dtypes.bfloat16).astype(np.float64), axis, -1)
    blocks = v.reshape(v.shape[:-1] + (-1, 32))
    amax = np.abs(blocks).max(-1, keepdims=True)
    byte = np.maximum(np.where(amax > 0, np.frexp(amax)[1] - 1 + 127, 0) - down, 1)
    scale = np.exp2(byte - 127.0)
    codes = (blocks / scale).astype(np.float32).astype(dtype).astype(np.float64)
    return np.moveaxis((codes * scale).reshape(v.shape), -1, axis)


WIDE = False


def mx_kscale(k):
    if not WIDE:
        return np.ones(k)
    levels = np.array([30, -30])
    if k % 512:
        return np.exp2(np.random.permutation(np.resize(levels, k // 32))).repeat(32)
    a = np.empty((k // 512, 16))
    for p in range(k // 512):
        a[p, :8] = np.random.permutation(np.resize(levels, 8))
        for g in range(8):
            far = levels[np.abs(levels - a[p, g]) >= 10]
            a[p, g + 8] = far[np.random.randint(len(far))]
    return np.exp2(a.ravel()).repeat(32)


def f64(x):
    return np.asarray(x).astype(np.float64)


def striped(idx):
    return np.tile(np.asarray(idx).reshape(-1, 16).T, (8, 1)).astype(np.uint16)


def unstriped(offs):
    return offs[:16].T.reshape(-1).astype(np.int64)


E2M1 = np.array([0.0, 0.5, 1.0, 1.5, 2.0, 3.0, 4.0, 6.0, -0.0, -0.5, -1.0, -1.5, -2.0, -3.0, -4.0, -6.0])


def pack_weight(w, fmt):
    k, n = w.shape
    w = f64(np.asarray(w, np.float32).astype(ml_dtypes.bfloat16)).reshape(k // 32, 32, n)
    amax = np.abs(w).max(1)
    if fmt == "e4m3":
        byte = np.frexp(amax)[1] - 1 + 127 - 7
    else:
        mant, ex = np.frexp(amax / 6.0)
        byte = np.where(mant > 0.5, ex, ex - 1) + 127
    byte = np.clip(np.where(amax > 0, byte, 1), 1, 254)
    scaled = (w * np.exp2(127.0 - byte)[:, None, :]).reshape(k, n).astype(np.float32)
    by_word = np.ascontiguousarray(scaled.reshape(k // 512, 128, 4, n).transpose(0, 1, 3, 2))
    if fmt == "e4m3":
        words = by_word.astype(ml_dtypes.float8_e4m3fn).view(np.uint8)
    else:
        c = by_word.astype(ml_dtypes.float4_e2m1fn).view(np.uint8) & 0xF
        words = (c[..., 0::2] | (c[..., 1::2] << 4)).reshape(k // 512, 128, 2 * n)
    return np.ascontiguousarray(words), np.ascontiguousarray(byte.astype(np.uint8).reshape(k // 512, 16, n))


def unpack_weight(words, scales, fmt):
    g, _, n = scales.shape
    words = np.ascontiguousarray(words).reshape(g, 128, n, -1)
    if fmt == "e4m3":
        vals = words.view(ml_dtypes.float8_e4m3fn).astype(np.float64)
    else:
        nib = np.empty((g, 128, n, 4), np.uint8)
        nib[..., 0::2] = words & 0xF
        nib[..., 1::2] = words >> 4
        vals = E2M1[nib]
    vals = vals * np.repeat(np.exp2(scales.astype(np.float64) - 127.0), 8, axis=1)[..., None]
    return vals.transpose(0, 1, 3, 2).reshape(g * 512, n)


K, T, J, I, G = 1024, 1024, 256, 256, 32


def setup_inputs():
    n = np.random.standard_normal
    idx = np.random.permutation(T)[:J]
    fk = mx_kscale(K)
    kyp = pack_weight(n((K, I)) / fk[:, None], "e4m3")
    return {
        "xf": (n((K, T)) * 0.03).astype(np.float32),
        "fk": (np.random.uniform(0.5, 2.0, (K, 1)) * fk[:, None]).astype(np.float32),
        "ky_words": kyp[0],
        "ky_scales": kyp[1],
        "bi": (np.random.uniform(-0.7, 0.7, (1, I))).astype(np.float32),
        "offs": striped(idx),
    }


def reference(xf, fk, ky_words, ky_scales, bi, offs):
    idx = unstriped(offs)
    kyu = unpack_weight(ky_words, ky_scales, "e4m3")
    xg = f64(xf)[:, idx]
    x1 = np.pad(xg, ((0, 0), (1, 0)))[:, :J]
    u = (xg - 0.6 * x1) * f64(fk)
    uq = mxq(u, 0, "e5m2")
    a0 = uq.T @ kyu
    a = a0 + f64(bi)
    g1 = a.reshape(J, G, I // G).max(axis=2)
    y = g1 - 0.5 * np.max(a, axis=1, keepdims=True)
    return y

@@ -1,0 +1,161 @@
+from contextlib import ExitStack
+
+import concourse.mybir as mybir
+from concourse.masks import make_identity
+
+K, T, J, I, G = 1024, 1024, 256, 256, 32
+FLOPS = 2 * K * J * I
+
+F32 = mybir.dt.float32
+BF16 = mybir.dt.bfloat16
+U32 = mybir.dt.uint32
+I32 = mybir.dt.int32
+U16 = mybir.dt.uint16
+U8 = mybir.dt.uint8
+E4M3X4 = mybir.dt.float8_e4m3fn_x4
+E5M2X4 = mybir.dt.float8_e5m2_x4
+ALU = mybir.AluOpType
+COPY = mybir.ActivationFunctionType.Copy
+AXIS_X = mybir.AxisListType.X
+
+P = 128
+PACK = 4
+PASSES = K // (P * PACK)
+HALVES = J // P
+PAD = 8
+BUNDLE = I // G
+LIST_GROUP = 16
+FINE_PLANES = 2
+
+
+def tile_list_scores_steps_given_bundles_kernel(tc, xf, fk, ky_words, ky_scales, bi, offs, out):
+    nc = tc.nc
+    with ExitStack() as ctx:
+        keep = ctx.enter_context(tc.tile_pool(name="keep", bufs=1))
+        psum = ctx.enter_context(tc.psum_pool(name="psum", bufs=1))
+
+        offsets = keep.tile([P, J // LIST_GROUP], U16, name="offsets")
+        planes = [(a, t) for a in range(PASSES) for t in range(PACK)]
+        x_rows = xf.rearrange("(a p t) n -> a t p n", a=PASSES, t=PACK)
+        window = {}
+        for n, (a, t) in enumerate(planes):
+            window[a, t] = keep.tile([P, T], F32, name="window_%d_%d" % (a, t))
+            nc.sync.dma_start(window[a, t][:], x_rows[a, t])
+            if n == 0:
+                nc.sync.dma_start(offsets[:], offs)
+        key_words = []
+        for a in range(PASSES):
+            words = keep.tile([P, I], U32, name="key_words_%d" % a, align_bytes=64)
+            nc.sync.dma_start(words[:].bitcast(I32), ky_words[a].rearrange("p n t -> p (n t)").bitcast(I32))
+            key_words.append(words)
+
+        identity = keep.tile([P, P], F32, name="identity")
+        make_identity(nc, identity[:])
+
+        factor = keep.tile([P, PASSES, PACK], F32, name="factor")
+        nc.scalar.dma_start(factor[:], fk.rearrange("(a p t) o -> p a (t o)", a=PASSES, t=PACK))
+        bias_col = keep.tile([P, HALVES], F32, name="bias_col")
+        nc.scalar.dma_start(bias_col[:], bi.rearrange("o (p c) -> p (o c)", c=HALVES))
+        key_scales = keep.tile([P, PASSES, I], U8, name="key_scales", align_bytes=64)
+        nc.vector.memset(key_scales[:].bitcast(I32), 0)
+        for q in range(4):
+            nc.gpsimd.dma_start(
+                key_scales[32 * q : 32 * q + 4, :, :].bitcast(I32),
+                ky_scales[:, 4 * q : 4 * q + 4, :].rearrange("a r n -> r a n").bitcast(I32),
+            )
+
+        picked = keep.tile([P, len(planes), PAD + J], F32, name="picked")
+        nc.vector.memset(picked[:, :, 0:PAD], 0.0)
+
+        bias_psum = psum.tile([P, HALVES, P], F32, name="bias_psum")
+        for c in range(HALVES):
+            nc.tensor.transpose(bias_psum[:, c, :], bias_col[:, c : c + 1].to_broadcast([P, P]), identity[:])
+        bias = keep.tile([P, I], F32, name="bias")
+        nc.vector.tensor_copy(bias[:].rearrange("p (n c) -> p n c", c=HALVES), bias_psum[:].rearrange("p c n -> p n c"))
+
+        stepped = keep.tile([P, len(planes), J], F32, name="stepped")
+        rounded = [keep.tile([P, J, PACK], BF16, name="rounded_%d" % a, align_bytes=64) for a in range(PASSES)]
+        codes = [keep.tile([P, J], U32, name="codes_%d" % a, align_bytes=64) for a in range(PASSES)]
+        scales = [keep.tile([P, J], U8, name="scales_%d" % a, align_bytes=64) for a in range(PASSES)]
+        acc = [psum.tile([P, I], F32, name="acc_%d" % h) for h in range(HALVES)]
+
+        def gather(a, t, j0, j1):
+            nc.scalar.activation(
+                picked[:, a * PACK + t, PAD + j0 : PAD + j1],
+                window[a, t][:].indirect(offsets[:, j0 // LIST_GROUP : j1 // LIST_GROUP]),
+                COPY,
+            )
+
+        def step(a, t, j0, j1):
+            n = a * PACK + t
+            nc.vector.scalar_tensor_tensor(
+                out=stepped[:, n, j0:j1],
+                in0=picked[:, n, PAD - 1 + j0 : PAD - 1 + j1],
+                scalar=-0.6,
+                in1=picked[:, n, PAD + j0 : PAD + j1],
+                op0=ALU.mult,
+                op1=ALU.add,
+            )
+
+        def scale_and_round(a, t, j0, j1):
+            nc.vector.tensor_scalar(
+                out=rounded[a][:, j0:j1, t],
+                in0=stepped[:, a * PACK + t, j0:j1],
+                scalar1=factor[:, a, t : t + 1],
+                scalar2=None,
+                op0=ALU.mult,
+            )
+
+        def quantise(a, j0, j1):
+            nc.vector.quantize_mx(
+                out=codes[a][:, j0:j1].bitcast(E5M2X4),
+                scales=scales[a][:, j0:j1],
+                in_=rounded[a][:, j0:j1, :].rearrange("p j t -> p (j t)"),
+            )
+
+        def multiply(a, h):
+            rows = slice(h * P, (h + 1) * P)
+            nc.tensor.matmul_mx(
+                out=acc[h][:],
+                lhsT=codes[a][:, rows].bitcast(E5M2X4),
+                lhsT_scale=scales[a][:, rows],
+                rhs=key_words[a][:].bitcast(E4M3X4),
+                rhs_scale=key_scales[:, a, :],
+                start=(a == 0),
+                stop=(a == PASSES - 1),
+            )
+
+        whole = [(0, J)]
+        halves = [(h * P, (h + 1) * P) for h in range(HALVES)]
+        for n, (a, t) in enumerate(planes):
+            pieces = halves if n >= len(planes) - FINE_PLANES else whole
+            for stage in (gather, step, scale_and_round):
+                for j0, j1 in pieces:
+                    stage(a, t, j0, j1)
+            if t == PACK - 1:
+                for j0, j1 in pieces:
+                    quantise(a, j0, j1)
+                for h in range(HALVES):
+                    multiply(a, h)
+
+        score = [keep.tile([P, G, BUNDLE], F32, name="score_%d" % h) for h in range(HALVES)]
+        best = [keep.tile([P, G], F32, name="best_%d" % h) for h in range(HALVES)]
+        top = [keep.tile([P, 1], F32, name="top_%d" % h) for h in range(HALVES)]
+        result = [keep.tile([P, G], F32, name="result_%d" % h) for h in range(HALVES)]
+        for h in range(HALVES):
+            nc.vector.tensor_tensor(score[h][:].rearrange("p g b -> p (g b)"), acc[h][:], bias[:], ALU.add)
+        for h in range(HALVES):
+            nc.vector.tensor_reduce(best[h][:], score[h][:], AXIS_X, ALU.max)
+        for h in range(HALVES):
+            nc.vector.tensor_reduce(top[h][:], best[h][:], AXIS_X, ALU.max)
+        for h in range(HALVES):
+            nc.vector.scalar_tensor_tensor(
+                out=result[h][:],
+                in0=top[h][:].to_broadcast([P, G]),
+                scalar=-0.5,
+                in1=best[h][:],
+                op0=ALU.mult,
+                op1=ALU.add,
+            )
+            queue = nc.scalar if h == 0 else nc.sync
+            queue.dma_start(out[h * P : (h + 1) * P, :], result[h][:])

@@ -25,7 +25,6 @@ HALVES = J // P
 PAD = 8
 BUNDLE = I // G
 LIST_GROUP = 16
-FINE_PLANES = 2
 
 
 def tile_list_scores_steps_given_bundles_kernel(tc, xf, fk, ky_words, ky_scales, bi, offs, out):
@@ -43,6 +42,14 @@ def tile_list_scores_steps_given_bundles_kernel(tc, xf, fk, ky_words, ky_scales,
             nc.sync.dma_start(window[a, t][:], x_rows[a, t])
             if n == 0:
                 nc.sync.dma_start(offsets[:], offs)
+        key_scales = keep.tile([P, PASSES, I], U8, name="key_scales", align_bytes=64)
+        nc.vector.memset(key_scales[:].bitcast(I32), 0)
+        for q in range(4):
+            nc.sync.dma_start(
+                key_scales[32 * q : 32 * q + 4, :, :].bitcast(I32),
+                ky_scales[:, 4 * q : 4 * q + 4, :].rearrange("a r n -> r a n").bitcast(I32),
+            )
+
         key_words = []
         for a in range(PASSES):
             words = keep.tile([P, I], U32, name="key_words_%d" % a, align_bytes=64)
@@ -56,16 +63,10 @@ def tile_list_scores_steps_given_bundles_kernel(tc, xf, fk, ky_words, ky_scales,
         nc.scalar.dma_start(factor[:], fk.rearrange("(a p t) o -> p a (t o)", a=PASSES, t=PACK))
         bias_col = keep.tile([P, HALVES], F32, name="bias_col")
         nc.scalar.dma_start(bias_col[:], bi.rearrange("o (p c) -> p (o c)", c=HALVES))
-        key_scales = keep.tile([P, PASSES, I], U8, name="key_scales", align_bytes=64)
-        nc.vector.memset(key_scales[:].bitcast(I32), 0)
-        for q in range(4):
-            nc.gpsimd.dma_start(
-                key_scales[32 * q : 32 * q + 4, :, :].bitcast(I32),
-                ky_scales[:, 4 * q : 4 * q + 4, :].rearrange("a r n -> r a n").bitcast(I32),
-            )
-
         picked = keep.tile([P, len(planes), PAD + J], F32, name="picked")
-        nc.vector.memset(picked[:, :, 0:PAD], 0.0)
+        zeros = keep.tile([P, len(planes), PAD], F32, name="zeros")
+        nc.vector.memset(zeros[:], 0.0)
+        nc.scalar.activation(picked[:, :, 0:PAD], zeros[:], COPY)
 
         bias_psum = psum.tile([P, HALVES, P], F32, name="bias_psum")
         for c in range(HALVES):
@@ -79,28 +80,29 @@ def tile_list_scores_steps_given_bundles_kernel(tc, xf, fk, ky_words, ky_scales,
         scales = [keep.tile([P, J], U8, name="scales_%d" % a, align_bytes=64) for a in range(PASSES)]
         acc = [psum.tile([P, I], F32, name="acc_%d" % h) for h in range(HALVES)]
 
-        def gather(a, t, j0, j1):
+        def gather(a, t, h):
+            cols = P // LIST_GROUP
             nc.scalar.activation(
-                picked[:, a * PACK + t, PAD + j0 : PAD + j1],
-                window[a, t][:].indirect(offsets[:, j0 // LIST_GROUP : j1 // LIST_GROUP]),
+                picked[:, a * PACK + t, PAD + h * P : PAD + (h + 1) * P],
+                window[a, t][:].indirect(offsets[:, h * cols : (h + 1) * cols]),
                 COPY,
             )
 
-        def step(a, t, j0, j1):
+        def step(a, t, h):
             n = a * PACK + t
             nc.vector.scalar_tensor_tensor(
-                out=stepped[:, n, j0:j1],
-                in0=picked[:, n, PAD - 1 + j0 : PAD - 1 + j1],
+                out=stepped[:, n, h * P : (h + 1) * P],
+                in0=picked[:, n, PAD - 1 + h * P : PAD - 1 + (h + 1) * P],
                 scalar=-0.6,
-                in1=picked[:, n, PAD + j0 : PAD + j1],
+                in1=picked[:, n, PAD + h * P : PAD + (h + 1) * P],
                 op0=ALU.mult,
                 op1=ALU.add,
             )
 
-        def scale_and_round(a, t, j0, j1):
+        def scale_and_round(a, t, h):
             nc.vector.tensor_scalar(
-                out=rounded[a][:, j0:j1, t],
-                in0=stepped[:, a * PACK + t, j0:j1],
+                out=rounded[a][:, h * P : (h + 1) * P, t],
+                in0=stepped[:, a * PACK + t, h * P : (h + 1) * P],
                 scalar1=factor[:, a, t : t + 1],
                 scalar2=None,
                 op0=ALU.mult,
@@ -125,17 +127,13 @@ def tile_list_scores_steps_given_bundles_kernel(tc, xf, fk, ky_words, ky_scales,
                 stop=(a == PASSES - 1),
             )
 
-        whole = [(0, J)]
-        halves = [(h * P, (h + 1) * P) for h in range(HALVES)]
-        for n, (a, t) in enumerate(planes):
-            pieces = halves if n >= len(planes) - FINE_PLANES else whole
+        for a, t in planes:
             for stage in (gather, step, scale_and_round):
-                for j0, j1 in pieces:
-                    stage(a, t, j0, j1)
-            if t == PACK - 1:
-                for j0, j1 in pieces:
-                    quantise(a, j0, j1)
                 for h in range(HALVES):
+                    stage(a, t, h)
+            if t == PACK - 1:
+                for h in range(HALVES):
+                    quantise(a, h * P, (h + 1) * P)
                     multiply(a, h)
 
         score = [keep.tile([P, G, BUNDLE], F32, name="score_%d" % h) for h in range(HALVES)]

from contextlib import ExitStack

import concourse.mybir as mybir
from concourse.masks import make_identity

K, T, J, I, G = 1024, 1024, 256, 256, 32
FLOPS = 2 * K * J * I

F32 = mybir.dt.float32
BF16 = mybir.dt.bfloat16
U32 = mybir.dt.uint32
I32 = mybir.dt.int32
U16 = mybir.dt.uint16
U8 = mybir.dt.uint8
E4M3X4 = mybir.dt.float8_e4m3fn_x4
E5M2X4 = mybir.dt.float8_e5m2_x4
ALU = mybir.AluOpType
COPY = mybir.ActivationFunctionType.Copy
AXIS_X = mybir.AxisListType.X

P = 128
PACK = 4
PASSES = K // (P * PACK)
HALVES = J // P
PAD = 8
BUNDLE = I // G
LIST_GROUP = 16


def tile_list_scores_steps_given_bundles_kernel(tc, xf, fk, ky_words, ky_scales, bi, offs, out):
    nc = tc.nc
    with ExitStack() as ctx:
        keep = ctx.enter_context(tc.tile_pool(name="keep", bufs=1))
        psum = ctx.enter_context(tc.psum_pool(name="psum", bufs=1))

        offsets = keep.tile([P, J // LIST_GROUP], U16, name="offsets")
        planes = [(a, t) for a in range(PASSES) for t in range(PACK)]
        x_rows = xf.rearrange("(a p t) n -> a t p n", a=PASSES, t=PACK)
        window = {}
        for n, (a, t) in enumerate(planes):
            window[a, t] = keep.tile([P, T], F32, name="window_%d_%d" % (a, t))
            nc.sync.dma_start(window[a, t][:], x_rows[a, t])
            if n == 0:
                nc.sync.dma_start(offsets[:], offs)
        key_scales = keep.tile([P, PASSES, I], U8, name="key_scales", align_bytes=64)
        nc.vector.memset(key_scales[:].bitcast(I32), 0)
        for q in range(4):
            nc.sync.dma_start(
                key_scales[32 * q : 32 * q + 4, :, :].bitcast(I32),
                ky_scales[:, 4 * q : 4 * q + 4, :].rearrange("a r n -> r a n").bitcast(I32),
            )

        key_words = []
        for a in range(PASSES):
            words = keep.tile([P, I], U32, name="key_words_%d" % a, align_bytes=64)
            nc.sync.dma_start(words[:].bitcast(I32), ky_words[a].rearrange("p n t -> p (n t)").bitcast(I32))
            key_words.append(words)

        identity = keep.tile([P, P], F32, name="identity")
        make_identity(nc, identity[:])

        factor = keep.tile([P, PASSES, PACK], F32, name="factor")
        nc.scalar.dma_start(factor[:], fk.rearrange("(a p t) o -> p a (t o)", a=PASSES, t=PACK))
        bias_col = keep.tile([P, HALVES], F32, name="bias_col")
        nc.scalar.dma_start(bias_col[:], bi.rearrange("o (p c) -> p (o c)", c=HALVES))
        picked = keep.tile([P, len(planes), PAD + J], F32, name="picked")
        zeros = keep.tile([P, len(planes), PAD], F32, name="zeros")
        nc.vector.memset(zeros[:], 0.0)
        nc.scalar.activation(picked[:, :, 0:PAD], zeros[:], COPY)

        bias_psum = psum.tile([P, HALVES, P], F32, name="bias_psum")
        for c in range(HALVES):
            nc.tensor.transpose(bias_psum[:, c, :], bias_col[:, c : c + 1].to_broadcast([P, P]), identity[:])
        bias = keep.tile([P, I], F32, name="bias")
        nc.vector.tensor_copy(bias[:].rearrange("p (n c) -> p n c", c=HALVES), bias_psum[:].rearrange("p c n -> p n c"))

        stepped = keep.tile([P, len(planes), J], F32, name="stepped")
        rounded = [keep.tile([P, J, PACK], BF16, name="rounded_%d" % a, align_bytes=64) for a in range(PASSES)]
        codes = [keep.tile([P, J], U32, name="codes_%d" % a, align_bytes=64) for a in range(PASSES)]
        scales = [keep.tile([P, J], U8, name="scales_%d" % a, align_bytes=64) for a in range(PASSES)]
        acc = [psum.tile([P, I], F32, name="acc_%d" % h) for h in range(HALVES)]

        def gather(a, t, h):
            cols = P // LIST_GROUP
            nc.scalar.activation(
                picked[:, a * PACK + t, PAD + h * P : PAD + (h + 1) * P],
                window[a, t][:].indirect(offsets[:, h * cols : (h + 1) * cols]),
                COPY,
            )

        def step(a, t, h):
            n = a * PACK + t
            nc.vector.scalar_tensor_tensor(
                out=stepped[:, n, h * P : (h + 1) * P],
                in0=picked[:, n, PAD - 1 + h * P : PAD - 1 + (h + 1) * P],
                scalar=-0.6,
                in1=picked[:, n, PAD + h * P : PAD + (h + 1) * P],
                op0=ALU.mult,
                op1=ALU.add,
            )

        def scale_and_round(a, t, h):
            nc.vector.tensor_scalar(
                out=rounded[a][:, h * P : (h + 1) * P, t],
                in0=stepped[:, a * PACK + t, h * P : (h + 1) * P],
                scalar1=factor[:, a, t : t + 1],
                scalar2=None,
                op0=ALU.mult,
            )

        def quantise(a, j0, j1):
            nc.vector.quantize_mx(
                out=codes[a][:, j0:j1].bitcast(E5M2X4),
                scales=scales[a][:, j0:j1],
                in_=rounded[a][:, j0:j1, :].rearrange("p j t -> p (j t)"),
            )

        def multiply(a, h):
            rows = slice(h * P, (h + 1) * P)
            nc.tensor.matmul_mx(
                out=acc[h][:],
                lhsT=codes[a][:, rows].bitcast(E5M2X4),
                lhsT_scale=scales[a][:, rows],
                rhs=key_words[a][:].bitcast(E4M3X4),
                rhs_scale=key_scales[:, a, :],
                start=(a == 0),
                stop=(a == PASSES - 1),
            )

        for a, t in planes:
            for stage in (gather, step, scale_and_round):
                for h in range(HALVES):
                    stage(a, t, h)
            if t == PACK - 1:
                for h in range(HALVES):
                    quantise(a, h * P, (h + 1) * P)
                    multiply(a, h)

        score = [keep.tile([P, G, BUNDLE], F32, name="score_%d" % h) for h in range(HALVES)]
        best = [keep.tile([P, G], F32, name="best_%d" % h) for h in range(HALVES)]
        top = [keep.tile([P, 1], F32, name="top_%d" % h) for h in range(HALVES)]
        result = [keep.tile([P, G], F32, name="result_%d" % h) for h in range(HALVES)]
        for h in range(HALVES):
            nc.vector.tensor_tensor(score[h][:].rearrange("p g b -> p (g b)"), acc[h][:], bias[:], ALU.add)
        for h in range(HALVES):
            nc.vector.tensor_reduce(best[h][:], score[h][:], AXIS_X, ALU.max)
        for h in range(HALVES):
            nc.vector.tensor_reduce(top[h][:], best[h][:], AXIS_X, ALU.max)
        for h in range(HALVES):
            nc.vector.scalar_tensor_tensor(
                out=result[h][:],
                in0=top[h][:].to_broadcast([P, G]),
                scalar=-0.5,
                in1=best[h][:],
                op0=ALU.mult,
                op1=ALU.add,
            )
            queue = nc.scalar if h == 0 else nc.sync
            queue.dma_start(out[h * P : (h + 1) * P, :], result[h][:])
